import numpy as np, ml_dtypes
CORES = [144,200,272,328,400,456]
N = 6
import mx_ref
NC, WB = 128, 2
D = 2 * WB + 1
BF = ml_dtypes.bfloat16
def setup_inputs(rng):
    def f(*shape):
        return mx_ref.flush((rng.standard_normal(shape, dtype=np.float32) * np.exp2(rng.integers(-2, 3, shape[:-1] + (1,)))).astype(BF))
    return {"w": f(N, 128, D * 512), "x": f(N, 128, 4 * NC)}
def setup_inputs_blocks(rng):
    d = setup_inputs(rng)
    for k in ("w", "x"): d[k] = mx_ref.spread(d[k], rng, 2)
    return d
def setup_inputs_wide(rng):
    d = setup_inputs(rng)
    for k in ("w", "x"): d[k] = mx_ref.flush((d[k].astype(np.float32) * np.exp2(rng.integers(-8, 9, (N, 1, 1))).astype(np.float32)).astype(BF))
    return d
def setup_inputs_zeros(rng):
    d = setup_inputs(rng); v = d["x"].reshape(N, 128, -1, 4).copy()
    v[np.broadcast_to((rng.random((N, 1, v.shape[2], 1)) < 0.33), v.shape)] = 0
    d["x"] = v.reshape(d["x"].shape)
    return d
def reference(w, x):
    QX = [mx_ref.quantize(x[j]) for j in range(N)]
    y = np.zeros((N, 128, NC), np.float32)
    for r in range(N):
        for i in range(D):
            p = mx_ref.matmul(mx_ref.quantize(w[r][:, 512 * i:512 * i + 512]), QX[(r + i - WB) % N])
            y[r] = p if i == 0 else y[r] + p
    return {"y": y}

from concourse.bass import DstId, RemoteDMATransfer
from concourse.mybir import dt

N, WB, NC = 6, 2, 128
D = 2 * WB + 1
HOSTS = 4
PER_CALL = 2
EARLY = (2, 4)

SCRATCH = {
    "xb": ("sbuf", [128, 4 * NC], "bfloat16"),
    "wb": ("sbuf", [128, 4 * NC * D], "bfloat16"),
    "wq": ("sbuf", [128, NC * D], "float8_e4m3fn_x4"),
    "ws": ("sbuf", [128, NC * D], "uint8"),
    "xq": ("sbuf", [128, NC * D], "float8_e4m3fn_x4"),
    "xs": ("sbuf", [128, NC * D], "uint8"),
    "yo": ("sbuf", [128, NC], "float32"),
    "ps": ("psum", [128, 512], "float32"),
}
SEMAPHORES = (["ldx", "lw0", "lw1", "lw2", "qx", "first", "sent", "mm", "cp", "st"]
              + ["qw%d" % i for i in range(D)] + ["S%d" % i for i in range(D)] + ["C%d" % i for i in range(D)])

_CACHE = {}


def _bits(mask):
    return [b for b in range(mask.bit_length()) if (mask >> b) & 1]


def _deal(pool, n):
    per = 1
    while per * 2 * n <= len(pool):
        per *= 2
    stride = len(pool) // per
    return [sum(1 << b for b in pool[k::stride][:per]) for k in range(n)]


def _plan(ranks, topo):
    world = range(HOSTS * topo.CORES_PER_HOST)
    place = lambda c: (topo.host(c), topo.chip(c))
    on = {}
    for c in world:
        on.setdefault(place(c), []).append(c)

    def links(a, b):
        if place(a) == place(b):
            return 0
        if topo.rack(topo.host(a)) != topo.rack(topo.host(b)):
            return 1 + links(a, on[(topo.host(a), topo.chip(b))][0])
        return 1 if (topo.same_plane(a, b) or topo.mates(a, b)) else 2

    reach = {c: sum(1 for r in ranks if r != c and topo.may_write(c, r)) for c in world}
    used = set(ranks)
    direct, via, cls = {}, {}, {}
    for pas in (0, 1):
        for j, src in enumerate(ranks):
            for k in range(-WB, WB + 1):
                d = (j + k) % N
                dst = ranks[d]
                if k == 0:
                    cls[(d, j)] = (0, 0, 0)
                    continue
                if topo.may_write(src, dst):
                    if pas == 0:
                        direct.setdefault(j, []).append(d)
                        cls[(d, j)] = (1, 0, links(src, dst))
                    continue
                cand = [c for c in world if c not in used and topo.may_write(src, c) and topo.may_write(c, dst)]
                least = min(reach[c] for c in cand)
                if (least == min(reach.values())) != (pas == 0):
                    continue
                if (d, j) in cls:
                    continue
                h = min(cand, key=lambda c: (links(src, c) + links(c, dst), links(src, c),
                                             topo.rack(topo.host(c)) != topo.rack(topo.host(src)),
                                             topo.die(c) != topo.die(src), reach[c], c))
                used.add(h)
                via.setdefault(j, []).append((h, d))
                cls[(d, j)] = (2, links(src, h), links(h, dst))

    calls, expect = {}, {}

    def call(core, piece, slot, wait, dsts):
        off = [x for x in dsts if place(x[0]) != place(core)]
        loc = [x for x in dsts if place(x[0]) == place(core)]
        out = []
        offpool = _bits(topo.mask(core, off[0][0])) if off else []
        if off:
            out += list(zip(off, _deal(offpool, len(off))))
        if loc:
            pool = [b for b in _bits(topo.mask(core, loc[0][0])) if b not in offpool]
            out += list(zip(loc, _deal(pool, len(loc))))
        trs = []
        for (dc, ds), m in out:
            trs.append((dc, ds, m))
            expect[(dc, ds, piece)] = len(_bits(m))
        calls.setdefault(core, []).append((piece, slot, wait, trs))

    for j, src in enumerate(ranks):
        helpers = [(h, 0) for h, d in via.get(j, [])]
        straight = [(ranks[d], (j - d + WB) % N) for d in direct.get(j, [])]
        off = [x for x in helpers if place(x[0]) != place(src)] + straight
        loc = [x for x in helpers if place(x[0]) == place(src)]
        rounds = [off[:PER_CALL] + loc[:PER_CALL]]
        off, loc = off[PER_CALL:], loc[PER_CALL:]
        while off or loc:
            rounds.append(off[:PER_CALL] + loc[:PER_CALL])
            off, loc = off[PER_CALL:], loc[PER_CALL:]
        for dsts in rounds:
            for piece in "SC":
                call(src, piece, WB, None, dsts)
    for j in range(N):
        for h, d in via.get(j, []):
            for piece in "SC":
                call(h, piece, 0, (piece + "0", expect[(h, 0, piece)]), [(ranks[d], (j - d + WB) % N)])
    order = {}
    for d in range(N):
        js = sorted(((d + k) % N for k in range(-WB, WB + 1)), key=lambda j: cls[(d, j)])
        order[d] = [(j - d + WB) % N for j in js]
    return calls, expect, order


def _send(g, core, T, topo, piece, slot, trs, local_sem):
    out = []
    for dc, ds, m in trs:
        rid, pid = topo.addr(dc, core)
        a, b = slot * NC, ds * NC
        if piece == "S":
            src, dst = T.xs[:, a:a + NC], T.xs[:, b:b + NC]
        else:
            src, dst = T.xq[:, a:a + NC].bitcast(dt.uint8), T.xq[:, b:b + NC].bitcast(dt.uint8)
        out.append(RemoteDMATransfer(dst_ids=[DstId(rid=rid, pnc=pid)], dma_engine_mask=m,
                                     remote_sem=T.sem["%s%d" % (piece, ds)], src=src, dst=dst))
    g.remote_dma_fused(out, local_sem=local_sem)
    return sum(len(_bits(m)) for _, _, m in trs)


def rank_program(g, core, T, topo):
    if "plan" not in _CACHE:
        _CACHE["plan"] = _plan(list(T.cores), topo)
    calls, expect, order = _CACHE["plan"]
    if core not in calls:
        return
    sem = T.sem
    rank = T.rank_of(core)

    if rank is None:
        left = 0
        for piece, slot, wait, trs in calls[core]:
            g.wait_ge(sem[wait[0]], wait[1])
            left += _send(g, core, T, topo, piece, slot, trs, sem.sent)
        g.wait_ge(sem.sent, left)
        return

    W = 4 * NC
    own = slice(WB * NC, WB * NC + NC)
    g.sync.dma_start(T.xb[:], T.x[:]).then_inc(sem.ldx, 16)
    parts = [("lw0", EARLY[0], EARLY[1]), ("lw1", 0, EARLY[0]), ("lw2", EARLY[1], D)]
    g.sync.dma_start(T.wb[:, W * EARLY[0]:W * EARLY[1]], T.w[:, W * EARLY[0]:W * EARLY[1]]).then_inc(sem.lw0, 16)

    g.wait_ge(sem.qx, 1)
    first = left = 0
    for k, (piece, slot, wait, trs) in enumerate(calls[core]):
        if k == 0:
            first = _send(g, core, T, topo, piece, slot, trs, sem.first)
        else:
            left += _send(g, core, T, topo, piece, slot, trs, sem.sent)

    for q, (name, a, b) in zip((g.sync, g.scalar), parts[1:]):
        q.wait_ge(sem.first, first)
        q.dma_start(T.wb[:, W * a:W * b], T.w[:, W * a:W * b]).then_inc(sem[name], 16)

    v = g.vector
    v.wait_ge(sem.ldx, 16)
    v.quantize_mx(T.xq[:, own], T.xs[:, own], T.xb[:]).then_inc(sem.qx, 1)
    for name, a, b in parts:
        v.wait_ge(sem[name], 16)
        for i in range(a, b):
            v.quantize_mx(T.wq[:, NC * i:NC * i + NC], T.ws[:, NC * i:NC * i + NC],
                          T.wb[:, W * i:W * i + W]).then_inc(sem["qw%d" % i], 1)

    t = g.tensor
    seq = order[rank]
    for k, i in enumerate(seq):
        t.wait_ge(sem["qw%d" % i], 1)
        if i == WB:
            t.wait_ge(sem.qx, 1)
        else:
            t.wait_ge(sem["S%d" % i], expect[(core, i, "S")])
            t.wait_ge(sem["C%d" % i], expect[(core, i, "C")])
        c = slice(NC * i, NC * i + NC)
        mm = t.matmul_mx(T.ps[:, 0:NC], T.wq[:, c], T.ws[:, c], T.xq[:, c], T.xs[:, c], k == 0, k == len(seq) - 1)
    mm.then_inc(sem.mm, 1)

    v.wait_ge(sem.mm, 1)
    v.tensor_copy(T.yo[:], T.ps[:, 0:NC]).then_inc(sem.cp, 1)
    g.sync.wait_ge(sem.cp, 1)
    g.sync.dma_start(T.y[:], T.yo[:]).then_inc(sem.st, 16)
    g.sync.wait_ge(sem.st, 16)
    g.wait_ge(sem.sent, left)
